import numpy as np
import ml_dtypes


def mxq(x, axis, fmt="e4m3"):
    dtype, down = {"e4m3": (ml_dtypes.float8_e4m3fn, 7), "e5m2": (ml_dtypes.float8_e5m2, 14)}[fmt]
    v = np.moveaxis(np.asarray(x, np.float32).astype(ml_dtypes.bfloat16).astype(np.float64), axis, -1)
    blocks = v.reshape(v.shape[:-1] + (-1, 32))
    amax = np.abs(blocks).max(-1, keepdims=True)
    byte = np.maximum(np.where(amax > 0, np.frexp(amax)[1] - 1 + 127, 0) - down, 1)
    scale = np.exp2(byte - 127.0)
    codes = (blocks / scale).astype(np.float32).astype(dtype).astype(np.float64)
    return np.moveaxis((codes * scale).reshape(v.shape), -1, axis)


WIDE = False


def mx_kscale(k):
    if not WIDE:
        return np.ones(k)
    levels = np.array([30, -30])
    if k % 512:
        return np.exp2(np.random.permutation(np.resize(levels, k // 32))).repeat(32)
    a = np.empty((k // 512, 16))
    for p in range(k // 512):
        a[p, :8] = np.random.permutation(np.resize(levels, 8))
        for g in range(8):
            far = levels[np.abs(levels - a[p, g]) >= 10]
            a[p, g + 8] = far[np.random.randint(len(far))]
    return np.exp2(a.ravel()).repeat(32)


def f64(x):
    return np.asarray(x).astype(np.float64)


def striped(idx):
    return np.tile(np.asarray(idx).reshape(-1, 16).T, (8, 1)).astype(np.uint16)


def unstriped(offs):
    return offs[:16].T.reshape(-1).astype(np.int64)


E2M1 = np.array([0.0, 0.5, 1.0, 1.5, 2.0, 3.0, 4.0, 6.0, -0.0, -0.5, -1.0, -1.5, -2.0, -3.0, -4.0, -6.0])


def pack_weight(w, fmt):
    k, n = w.shape
    w = f64(np.asarray(w, np.float32).astype(ml_dtypes.bfloat16)).reshape(k // 32, 32, n)
    amax = np.abs(w).max(1)
    if fmt in ("e4m3", "e5m2"):
        byte = np.frexp(amax)[1] - 1 + 127 - (7 if fmt == "e4m3" else 14)
    else:
        mant, ex = np.frexp(amax / 6.0)
        byte = np.where(mant > 0.5, ex, ex - 1) + 127
    byte = np.clip(np.where(amax > 0, byte, 1), 1, 254)
    scaled = (w * np.exp2(127.0 - byte)[:, None, :]).reshape(k, n).astype(np.float32)
    by_word = np.ascontiguousarray(scaled.reshape(k // 512, 128, 4, n).transpose(0, 1, 3, 2))
    if fmt in ("e4m3", "e5m2"):
        words = by_word.astype(ml_dtypes.float8_e4m3fn if fmt == "e4m3" else ml_dtypes.float8_e5m2).view(np.uint8)
    else:
        c = by_word.astype(ml_dtypes.float4_e2m1fn).view(np.uint8) & 0xF
        words = (c[..., 0::2] | (c[..., 1::2] << 4)).reshape(k // 512, 128, 2 * n)
    return np.ascontiguousarray(words), np.ascontiguousarray(byte.astype(np.uint8).reshape(k // 512, 16, n))


def unpack_weight(words, scales, fmt):
    g, _, n = scales.shape
    words = np.ascontiguousarray(words).reshape(g, 128, n, -1)
    if fmt in ("e4m3", "e5m2"):
        vals = words.view(ml_dtypes.float8_e4m3fn if fmt == "e4m3" else ml_dtypes.float8_e5m2).astype(np.float64)
    else:
        nib = np.empty((g, 128, n, 4), np.uint8)
        nib[..., 0::2] = words & 0xF
        nib[..., 1::2] = words >> 4
        vals = E2M1[nib]
    vals = vals * np.repeat(np.exp2(scales.astype(np.float64) - 127.0), 8, axis=1)[..., None]
    return vals.transpose(0, 1, 3, 2).reshape(g * 512, n)


K, T, J, N, S, L = 1024, 1024, 256, 256, 512, 512


def setup_inputs():
    n = np.random.standard_normal
    idx = np.random.permutation(T)[:J]
    idx2 = np.random.permutation(S)[:J]
    fk = mx_kscale(K)
    fl = mx_kscale(L)
    xtp = pack_weight(n((K, T)) * np.random.uniform(0.4, 1.6, (1, T)) / fk[:, None], "e2m1")
    wap = pack_weight(n((K, N)) * 1 / np.sqrt(K) * fk[:, None], "e2m1")
    wbp = pack_weight(n((L, N)) * 1 / np.sqrt(L) * fl[:, None], "e5m2")
    return {
        "xt_words": xtp[0],
        "xt_scales": xtp[1],
        "wa_words": wap[0],
        "wa_scales": wap[1],
        "xs": (n((L, S)) * np.random.uniform(0.4, 1.6, (1, S)) / fl[:, None]).astype(np.float32),
        "wb_words": wbp[0],
        "wb_scales": wbp[1],
        "bi": (np.random.uniform(-0.6, 0.6, (1, N))).astype(np.float32),
        "rs": (1.0 * n((J, N))).astype(np.float32),
        "offs": striped(idx),
        "offs2": striped(idx2),
    }


def reference(xt_words, xt_scales, wa_words, wa_scales, xs, wb_words, wb_scales, bi, rs, offs, offs2):
    idx = unstriped(offs)
    idx2 = unstriped(offs2)
    xtu = unpack_weight(xt_words, xt_scales, "e2m1")
    wau = unpack_weight(wa_words, wa_scales, "e2m1")
    wbu = unpack_weight(wb_words, wb_scales, "e5m2")
    xtidxg = xtu[:, idx]
    a = xtidxg.T @ wau
    xsidx2q = mxq(f64(xs)[:, idx2], 0, "e5m2")
    b0 = xsidx2q.T @ wbu
    b2 = b0 + f64(bi)
    d = a - b2
    y = d / (np.max(np.abs(d), axis=1, keepdims=True) + 0.2) + 0.3 * f64(rs)
    return y

@@ -1,0 +1,163 @@
+from contextlib import ExitStack
+
+import concourse.mybir as mybir
+from concourse.masks import make_identity
+
+K, T, J, N, S, L = 1024, 1024, 256, 256, 512, 512
+FLOPS = 2 * J * N * (K + L)
+
+F32 = mybir.dt.float32
+BF16 = mybir.dt.bfloat16
+I32 = mybir.dt.int32
+U16 = mybir.dt.uint16
+U8 = mybir.dt.uint8
+FP4X4 = mybir.dt.float4_e2m1fn_x4
+E5M2X4 = mybir.dt.float8_e5m2_x4
+ALU = mybir.AluOpType
+COPY = mybir.ActivationFunctionType.Copy
+
+P = 128
+PACK = 4
+PASSES = K // (P * PACK)
+TILES = J // P
+
+
+def tile_list_rows_othertable_gapoverpeak_kernel(
+    tc, xt_words, xt_scales, wa_words, wa_scales, xs, wb_words, wb_scales, bi, rs, offs, offs2, out
+):
+    nc = tc.nc
+    with ExitStack() as ctx:
+        sb = ctx.enter_context(tc.tile_pool(name="sb", bufs=1))
+        ps = ctx.enter_context(tc.psum_pool(name="ps", bufs=1))
+
+        idx = sb.tile([P, J // 16], U16, name="idx")
+        idx2 = sb.tile([P, J // 16], U16, name="idx2")
+        xt_s = sb.tile([P, PASSES, T], U8, name="xt_s", align_bytes=64)
+        xt_w = [sb.tile([P, T], U16, name="xt_w%d" % z, align_bytes=64) for z in range(PASSES)]
+        xs_sb = [sb.tile([P, 2, S], F32, name="xs_sb%d" % h, align_bytes=64) for h in range(2)]
+        wa_w = sb.tile([P, PASSES, 2 * N], U8, name="wa_w", align_bytes=64)
+        wa_s = sb.tile([P, PASSES, N], U8, name="wa_s", align_bytes=64)
+        wb_w = sb.tile([P, N], I32, name="wb_w", align_bytes=64)
+        wb_s = sb.tile([P, 1, N], U8, name="wb_s", align_bytes=64)
+        bi_col = sb.tile([P, 2], F32, name="bi_col")
+        rs_sb = sb.tile([P, TILES, N], F32, name="rs_sb")
+        ident = sb.tile([P, P], F32, name="ident")
+
+        nc.vector.memset(xt_s[:].bitcast(I32), 0)
+        nc.gpsimd.memset(wa_s[:].bitcast(I32), 0)
+        nc.vector.memset(wb_s[:].bitcast(I32), 0)
+
+        def load_scales(eng, plane, scales):
+            rows = scales.rearrange("z (q r) c -> r q z c", r=4)
+            for r in range(4):
+                eng.dma_start(out=plane[r:P:32].bitcast(I32), in_=rows[r].bitcast(I32))
+
+        xs_rows = xs.rearrange("(p t) s -> p t s", t=PACK)
+        for h in range(2):
+            nc.scalar.dma_start(out=xs_sb[h][:], in_=xs_rows[:, 2 * h : 2 * h + 2, :])
+        nc.sync.dma_start(idx2[:], offs2)
+        nc.sync.dma_start(idx[:], offs)
+        load_scales(nc.sync, xt_s, xt_scales)
+        for z in range(PASSES):
+            nc.sync.dma_start(out=xt_w[z][:].bitcast(I32), in_=xt_words[z].bitcast(I32))
+        nc.sync.dma_start(out=wa_w[:].bitcast(I32), in_=wa_words.rearrange("z p c -> p z c").bitcast(I32))
+        nc.sync.dma_start(out=bi_col[:], in_=bi[0].rearrange("(p c) -> p c", c=2))
+        load_scales(nc.sync, wb_s, wb_scales)
+        nc.sync.dma_start(out=wb_w[:], in_=wb_words[0].rearrange("p n t -> p (n t)").bitcast(I32))
+        nc.sync.dma_start(out=rs_sb[:], in_=rs.rearrange("(i p) n -> p i n", p=P))
+
+        load_scales(nc.gpsimd, wa_s, wa_scales)
+        make_identity(nc, ident[:])
+
+        g_s = [sb.tile([P, J], U8, name="g_s%d" % z, align_bytes=64) for z in range(PASSES)]
+        g_w = [sb.tile([P, J], U16, name="g_w%d" % z, align_bytes=64) for z in range(PASSES)]
+        g_x = sb.tile([P, PACK, J], F32, name="g_x", align_bytes=64)
+        woven = [sb.tile([P, P, PACK], BF16, name="woven%d" % i, align_bytes=64) for i in range(TILES)]
+        q_w = [sb.tile([P, P], I32, name="q_w%d" % i, align_bytes=64) for i in range(TILES)]
+        q_s = [sb.tile([P, P], U8, name="q_s%d" % i, align_bytes=64) for i in range(TILES)]
+
+        nc.vector.tensor_copy(g_x[:, 1, :], xs_sb[0][:, 1, :].indirect(idx2[:]))
+        for z in range(PASSES):
+            nc.vector.tensor_copy(g_s[z][:], xt_s[:, z, :].indirect(idx[:]))
+        for t in (0, 2, 3):
+            nc.scalar.activation(g_x[:, t, :], xs_sb[t // 2][:, t % 2, :].indirect(idx2[:]), COPY)
+        nc.vector.tensor_copy(g_w[0][:], xt_w[0][:].indirect(idx[:]))
+        for i in range(TILES):
+            nc.scalar.copy(
+                woven[i][:].rearrange("p (c u) t -> p c t u", u=4),
+                g_x[:, :, i * P : (i + 1) * P].rearrange("p t (c u) -> p c t u", u=4),
+            )
+
+        def quantise(i):
+            nc.vector.quantize_mx(
+                out=q_w[i][:].bitcast(E5M2X4), scales=q_s[i][:], in_=woven[i][:].rearrange("p c t -> p (c t)")
+            )
+
+        nc.vector.tensor_copy(g_w[1][:], xt_w[1][:].indirect(idx[:]))
+        quantise(0)
+        quantise(1)
+
+        bi_ps = ps.tile([P, 2, P], F32, name="bi_ps")
+        for c in range(2):
+            nc.tensor.transpose(bi_ps[:, c, :], bi_col[:, c : c + 1].to_broadcast([P, P]), ident[:])
+        bi_all = sb.tile([P, P, 2], F32, name="bi_all")
+        nc.scalar.copy(bi_all[:], bi_ps[:].rearrange("q c p -> q p c"))
+        rs3 = sb.tile([P, TILES, N], F32, name="rs3")
+        nc.scalar.activation(rs3[:], rs_sb[:], COPY, scale=0.3)
+
+        a_ps = [ps.tile([P, N], F32, name="a_ps%d" % i) for i in range(TILES)]
+        b_ps = [ps.tile([P, N], F32, name="b_ps%d" % i) for i in range(TILES)]
+
+        def pass_a(i, z):
+            nc.tensor.matmul_mx(
+                out=a_ps[i][:],
+                lhsT=g_w[z][:, i * P : (i + 1) * P].bitcast(FP4X4),
+                lhsT_scale=g_s[z][:, i * P : (i + 1) * P],
+                rhs=wa_w[:, z, :].bitcast(FP4X4),
+                rhs_scale=wa_s[:, z, :],
+                start=(z == 0),
+                stop=(z == PASSES - 1),
+            )
+
+        def pass_b(i):
+            nc.tensor.matmul_mx(
+                out=b_ps[i][:],
+                lhsT=q_w[i][:].bitcast(E5M2X4),
+                lhsT_scale=q_s[i][:],
+                rhs=wb_w[:].bitcast(E5M2X4),
+                rhs_scale=wb_s[:, 0, :],
+                start=True,
+                stop=True,
+            )
+
+        for z in range(PASSES):
+            for i in range(TILES):
+                pass_a(i, z)
+        for i in range(TILES):
+            pass_b(i)
+
+        b2 = [sb.tile([P, N], F32, name="b2_%d" % i) for i in range(TILES)]
+        d = [sb.tile([P, N], F32, name="d%d" % i) for i in range(TILES)]
+        y = [sb.tile([P, N], F32, name="y%d" % i) for i in range(TILES)]
+        peak = [sb.tile([P, 1], F32, name="peak%d" % i) for i in range(TILES)]
+        denom = [sb.tile([P, 1], F32, name="denom%d" % i) for i in range(TILES)]
+        inv = [sb.tile([P, 1], F32, name="inv%d" % i) for i in range(TILES)]
+
+        def steps(i):
+            return [
+                lambda: nc.vector.tensor_tensor(b2[i][:], a_ps[i][:], bi_all[:].rearrange("q p c -> q (p c)"), ALU.subtract),
+                lambda: nc.vector.tensor_tensor(d[i][:], b2[i][:], b_ps[i][:], ALU.subtract),
+                lambda: nc.vector.tensor_reduce(
+                    peak[i][:], d[i][:], mybir.AxisListType.X, ALU.max, apply_absolute_value=True
+                ),
+                lambda: nc.vector.tensor_scalar(denom[i][:], peak[i][:], 0.2, None, ALU.add),
+                lambda: nc.vector.reciprocal(inv[i][:], denom[i][:]),
+                lambda: nc.vector.scalar_tensor_tensor(
+                    y[i][:], d[i][:], inv[i][:], rs3[:, i, :], ALU.mult, ALU.add
+                ),
+                lambda: nc.sync.dma_start(out=out[i * P : (i + 1) * P, :], in_=y[i][:]),
+            ]
+
+        for first, second in zip(steps(0), steps(1)):
+            first()
+            second()

@@ -32,45 +32,51 @@ def tile_list_rows_othertable_gapoverpeak_kernel(
 
         idx = sb.tile([P, J // 16], U16, name="idx")
         idx2 = sb.tile([P, J // 16], U16, name="idx2")
-        xt_s = sb.tile([P, PASSES, T], U8, name="xt_s", align_bytes=64)
+        xt_s = sb.tile([P, PASSES, T], U8, name="xt_s", tag="reused", align_bytes=64)
         xt_w = [sb.tile([P, T], U16, name="xt_w%d" % z, align_bytes=64) for z in range(PASSES)]
         xs_sb = [sb.tile([P, 2, S], F32, name="xs_sb%d" % h, align_bytes=64) for h in range(2)]
         wa_w = sb.tile([P, PASSES, 2 * N], U8, name="wa_w", align_bytes=64)
-        wa_s = sb.tile([P, PASSES, N], U8, name="wa_s", align_bytes=64)
+        w_s = sb.tile([P, PASSES + 1, N], U8, name="w_s", align_bytes=64)
         wb_w = sb.tile([P, N], I32, name="wb_w", align_bytes=64)
-        wb_s = sb.tile([P, 1, N], U8, name="wb_s", align_bytes=64)
         bi_col = sb.tile([P, 2], F32, name="bi_col")
         rs_sb = sb.tile([P, TILES, N], F32, name="rs_sb")
         ident = sb.tile([P, P], F32, name="ident")
 
         nc.vector.memset(xt_s[:].bitcast(I32), 0)
-        nc.gpsimd.memset(wa_s[:].bitcast(I32), 0)
-        nc.vector.memset(wb_s[:].bitcast(I32), 0)
+        nc.vector.memset(ident[:], 0.0)
+        nc.vector.memset(w_s[:].bitcast(I32), 0)
 
-        def load_scales(eng, plane, scales):
+        def load_scale_row(eng, plane, scales, r):
             rows = scales.rearrange("z (q r) c -> r q z c", r=4)
-            for r in range(4):
-                eng.dma_start(out=plane[r:P:32].bitcast(I32), in_=rows[r].bitcast(I32))
+            eng.dma_start(out=plane[r:P:32].bitcast(I32), in_=rows[r].bitcast(I32))
 
         xs_rows = xs.rearrange("(p t) s -> p t s", t=PACK)
-        for h in range(2):
-            nc.scalar.dma_start(out=xs_sb[h][:], in_=xs_rows[:, 2 * h : 2 * h + 2, :])
+        nc.scalar.dma_start(out=xs_sb[0][:], in_=xs_rows[:, 0:2, :])
+        nc.gpsimd.dma_start(out=xs_sb[1][:], in_=xs_rows[:, 2:4, :])
+        make_identity(nc, ident[:], nomemset=True)
+        for z in range(PASSES):
+            nc.gpsimd.dma_start(out=xt_w[z][:].bitcast(I32), in_=xt_words[z].bitcast(I32))
+        nc.gpsimd.dma_start(out=wb_w[:], in_=wb_words[0].rearrange("p n t -> p (n t)").bitcast(I32))
+        nc.gpsimd.dma_start(out=rs_sb[:], in_=rs.rearrange("(i p) n -> p i n", p=P))
+
+        nc.sync.dma_start(out=bi_col[:], in_=bi[0].rearrange("(p c) -> p c", c=2))
         nc.sync.dma_start(idx2[:], offs2)
         nc.sync.dma_start(idx[:], offs)
-        load_scales(nc.sync, xt_s, xt_scales)
-        for z in range(PASSES):
-            nc.sync.dma_start(out=xt_w[z][:].bitcast(I32), in_=xt_words[z].bitcast(I32))
+        for r in range(4):
+            load_scale_row(nc.sync, xt_s, xt_scales, r)
         nc.sync.dma_start(out=wa_w[:].bitcast(I32), in_=wa_words.rearrange("z p c -> p z c").bitcast(I32))
-        nc.sync.dma_start(out=bi_col[:], in_=bi[0].rearrange("(p c) -> p c", c=2))
-        load_scales(nc.sync, wb_s, wb_scales)
-        nc.sync.dma_start(out=wb_w[:], in_=wb_words[0].rearrange("p n t -> p (n t)").bitcast(I32))
-        nc.sync.dma_start(out=rs_sb[:], in_=rs.rearrange("(i p) n -> p i n", p=P))
+        for r in range(4):
+            load_scale_row(nc.sync, w_s[:, 0:PASSES, :], wa_scales, r)
+        for r in range(4):
+            load_scale_row(nc.sync, w_s[:, PASSES : PASSES + 1, :], wb_scales, r)
 
-        load_scales(nc.gpsimd, wa_s, wa_scales)
-        make_identity(nc, ident[:])
+        bi_ps = ps.tile([P, 2, P], F32, name="bi_ps")
+        for c in range(2):
+            nc.tensor.transpose(bi_ps[:, c, :], bi_col[:, c : c + 1].to_broadcast([P, P]), ident[:])
+        bi_all = sb.tile([P, P, 2], F32, name="bi_all")
+        nc.scalar.activation(bi_all[:], bi_ps[:].rearrange("q c p -> q p c"), COPY)
 
         g_s = [sb.tile([P, J], U8, name="g_s%d" % z, align_bytes=64) for z in range(PASSES)]
-        g_w = [sb.tile([P, J], U16, name="g_w%d" % z, align_bytes=64) for z in range(PASSES)]
         g_x = sb.tile([P, PACK, J], F32, name="g_x", align_bytes=64)
         woven = [sb.tile([P, P, PACK], BF16, name="woven%d" % i, align_bytes=64) for i in range(TILES)]
         q_w = [sb.tile([P, P], I32, name="q_w%d" % i, align_bytes=64) for i in range(TILES)]
@@ -81,6 +87,10 @@ def tile_list_rows_othertable_gapoverpeak_kernel(
             nc.vector.tensor_copy(g_s[z][:], xt_s[:, z, :].indirect(idx[:]))
         for t in (0, 2, 3):
             nc.scalar.activation(g_x[:, t, :], xs_sb[t // 2][:, t % 2, :].indirect(idx2[:]), COPY)
+        g_w = [
+            sb.tile([P, J], U16, name="g_w0", tag="reused", align_bytes=64),
+            sb.tile([P, J], U16, name="g_w1", align_bytes=64),
+        ]
         nc.vector.tensor_copy(g_w[0][:], xt_w[0][:].indirect(idx[:]))
         for i in range(TILES):
             nc.scalar.copy(
@@ -97,11 +107,6 @@ def tile_list_rows_othertable_gapoverpeak_kernel(
         quantise(0)
         quantise(1)
 
-        bi_ps = ps.tile([P, 2, P], F32, name="bi_ps")
-        for c in range(2):
-            nc.tensor.transpose(bi_ps[:, c, :], bi_col[:, c : c + 1].to_broadcast([P, P]), ident[:])
-        bi_all = sb.tile([P, P, 2], F32, name="bi_all")
-        nc.scalar.copy(bi_all[:], bi_ps[:].rearrange("q c p -> q p c"))
         rs3 = sb.tile([P, TILES, N], F32, name="rs3")
         nc.scalar.activation(rs3[:], rs_sb[:], COPY, scale=0.3)
 
@@ -114,7 +119,7 @@ def tile_list_rows_othertable_gapoverpeak_kernel(
                 lhsT=g_w[z][:, i * P : (i + 1) * P].bitcast(FP4X4),
                 lhsT_scale=g_s[z][:, i * P : (i + 1) * P],
                 rhs=wa_w[:, z, :].bitcast(FP4X4),
-                rhs_scale=wa_s[:, z, :],
+                rhs_scale=w_s[:, z, :],
                 start=(z == 0),
                 stop=(z == PASSES - 1),
             )
@@ -125,7 +130,7 @@ def tile_list_rows_othertable_gapoverpeak_kernel(
                 lhsT=q_w[i][:].bitcast(E5M2X4),
                 lhsT_scale=q_s[i][:],
                 rhs=wb_w[:].bitcast(E5M2X4),
-                rhs_scale=wb_s[:, 0, :],
+                rhs_scale=w_s[:, PASSES, :],
                 start=True,
                 stop=True,
             )
@@ -158,6 +163,6 @@ def tile_list_rows_othertable_gapoverpeak_kernel(
                 lambda: nc.sync.dma_start(out=out[i * P : (i + 1) * P, :], in_=y[i][:]),
             ]
 
-        for first, second in zip(steps(0), steps(1)):
-            first()
-            second()
+        for i in range(TILES):
+            for step in steps(i):
+                step()

@@ -1,7 +1,6 @@
 from contextlib import ExitStack
 
 import concourse.mybir as mybir
-from concourse.masks import make_identity
 
 K, T, J, N, S, L = 1024, 1024, 256, 256, 512, 512
 FLOPS = 2 * J * N * (K + L)
@@ -14,7 +13,8 @@ U8 = mybir.dt.uint8
 FP4X4 = mybir.dt.float4_e2m1fn_x4
 E5M2X4 = mybir.dt.float8_e5m2_x4
 ALU = mybir.AluOpType
-COPY = mybir.ActivationFunctionType.Copy
+ACT = mybir.ActivationFunctionType
+COPY = ACT.Copy
 
 P = 128
 PACK = 4
@@ -32,43 +32,88 @@ def tile_list_rows_othertable_gapoverpeak_kernel(
 
         idx = sb.tile([P, J // 16], U16, name="idx")
         idx2 = sb.tile([P, J // 16], U16, name="idx2")
-        xt_s = sb.tile([P, PASSES, T], U8, name="xt_s", tag="reused", align_bytes=64)
-        xt_w = [sb.tile([P, T], U16, name="xt_w%d" % z, align_bytes=64) for z in range(PASSES)]
-        xs_sb = [sb.tile([P, 2, S], F32, name="xs_sb%d" % h, align_bytes=64) for h in range(2)]
+        xt_s = sb.tile([P, PASSES, T], U8, name="xt_s", align_bytes=64)
+        xt_w = [sb.tile([P, T], U16, name="xt_w%d" % z, tag="xt_w%d" % z, align_bytes=64) for z in range(PASSES)]
+        xs_sb = [sb.tile([P, 2, S], F32, name="xs_sb%d" % h, tag="xs_sb%d" % h, align_bytes=64) for h in range(2)]
         wa_w = sb.tile([P, PASSES, 2 * N], U8, name="wa_w", align_bytes=64)
-        w_s = sb.tile([P, PASSES + 1, N], U8, name="w_s", align_bytes=64)
+        wa_s = sb.tile([P, PASSES, N], U8, name="wa_s", align_bytes=64)
+        wb_s = sb.tile([P, 1, N], U8, name="wb_s", align_bytes=64)
         wb_w = sb.tile([P, N], I32, name="wb_w", align_bytes=64)
         bi_col = sb.tile([P, 2], F32, name="bi_col")
         rs_sb = sb.tile([P, TILES, N], F32, name="rs_sb")
+        zero = sb.tile([P, 1], F32, name="zero")
         ident = sb.tile([P, P], F32, name="ident")
 
         nc.vector.memset(xt_s[:].bitcast(I32), 0)
-        nc.vector.memset(ident[:], 0.0)
-        nc.vector.memset(w_s[:].bitcast(I32), 0)
+        nc.gpsimd.memset(zero[:], 0.0)
+        nc.gpsimd.memset(wa_s[:].bitcast(I32), 0)
+        nc.gpsimd.memset(wb_s[:].bitcast(I32), 0)
+        nc.scalar.activation(ident[:], zero[:].to_broadcast([P, P]), COPY)
+        ones = sb.tile([P, 32], F32, name="ones")
+        col = sb.tile([P, 32], F32, name="col", align_bytes=64)
+        row = sb.tile([P, 32], F32, name="row", align_bytes=64)
+        nc.vector.memset(ones[:], 1.0)
+        nc.vector.tensor_tensor_scan(col[:], ones[:], ones[:], 0.0, ALU.mult, ALU.add)
+        nc.vector.transpose(row[:], col[:])
+        for q in range(4):
+            part = slice(32 * q, 32 * q + 32)
+            nc.vector.tensor_tensor(ident[part, part], col[part, :], row[part, :], ALU.is_equal)
 
-        def load_scale_row(eng, plane, scales, r):
+        def load_scale_row(plane, scales, r):
             rows = scales.rearrange("z (q r) c -> r q z c", r=4)
-            eng.dma_start(out=plane[r:P:32].bitcast(I32), in_=rows[r].bitcast(I32))
+            nc.sync.dma_start(out=plane[r:P:32].bitcast(I32), in_=rows[r].bitcast(I32))
 
         xs_rows = xs.rearrange("(p t) s -> p t s", t=PACK)
         nc.scalar.dma_start(out=xs_sb[0][:], in_=xs_rows[:, 0:2, :])
-        nc.gpsimd.dma_start(out=xs_sb[1][:], in_=xs_rows[:, 2:4, :])
-        make_identity(nc, ident[:], nomemset=True)
-        for z in range(PASSES):
-            nc.gpsimd.dma_start(out=xt_w[z][:].bitcast(I32), in_=xt_words[z].bitcast(I32))
-        nc.gpsimd.dma_start(out=wb_w[:], in_=wb_words[0].rearrange("p n t -> p (n t)").bitcast(I32))
+        nc.gpsimd.dma_start(out=xt_w[0][:].bitcast(I32), in_=xt_words[0].bitcast(I32))
+        nc.gpsimd.dma_start(out=xt_w[1][:].bitcast(I32), in_=xt_words[1].bitcast(I32))
         nc.gpsimd.dma_start(out=rs_sb[:], in_=rs.rearrange("(i p) n -> p i n", p=P))
 
-        nc.sync.dma_start(out=bi_col[:], in_=bi[0].rearrange("(p c) -> p c", c=2))
         nc.sync.dma_start(idx2[:], offs2)
         nc.sync.dma_start(idx[:], offs)
         for r in range(4):
-            load_scale_row(nc.sync, xt_s, xt_scales, r)
+            load_scale_row(xt_s, xt_scales, r)
+        nc.sync.dma_start(out=xs_sb[1][:], in_=xs_rows[:, 2:4, :])
+        nc.sync.dma_start(out=bi_col[:], in_=bi[0].rearrange("(p c) -> p c", c=2))
+        for r in range(2):
+            load_scale_row(wa_s, wa_scales, r)
         nc.sync.dma_start(out=wa_w[:].bitcast(I32), in_=wa_words.rearrange("z p c -> p z c").bitcast(I32))
+        for r in range(2, 4):
+            load_scale_row(wa_s, wa_scales, r)
+        nc.sync.dma_start(out=wb_w[:], in_=wb_words[0].rearrange("p n t -> p (n t)").bitcast(I32))
         for r in range(4):
-            load_scale_row(nc.sync, w_s[:, 0:PASSES, :], wa_scales, r)
-        for r in range(4):
-            load_scale_row(nc.sync, w_s[:, PASSES : PASSES + 1, :], wb_scales, r)
+            load_scale_row(wb_s, wb_scales, r)
+
+        g_s = [sb.tile([P, J], U8, name="g_s%d" % z, align_bytes=64) for z in range(PASSES)]
+        g_x = sb.tile([P, PACK, J], F32, name="g_x", tag="g_x", align_bytes=64)
+        woven = [sb.tile([P, P, PACK], BF16, name="woven%d" % i, align_bytes=64) for i in range(TILES)]
+        q_s = [sb.tile([P, P], U8, name="q_s%d" % i, align_bytes=64) for i in range(TILES)]
+
+        for t in range(3):
+            nc.scalar.activation(g_x[:, t, :], xs_sb[t // 2][:, t % 2, :].indirect(idx2[:]), COPY)
+        for z in range(PASSES):
+            nc.vector.tensor_copy(g_s[z][:], xt_s[:, z, :].indirect(idx[:]))
+        nc.vector.tensor_copy(g_x[:, 3, :], xs_sb[1][:, 1, :].indirect(idx2[:]))
+        g_w = [sb.tile([P, J], U16, name="g_w0", tag="xs_sb1", align_bytes=64)]
+        nc.vector.tensor_copy(g_w[0][:], xt_w[0][:].indirect(idx[:]))
+        for i in range(TILES):
+            nc.scalar.activation(
+                woven[i][:].rearrange("p (c u) t -> p c t u", u=4),
+                g_x[:, :, i * P : (i + 1) * P].rearrange("p t (c u) -> p c t u", u=4),
+                COPY,
+                scale=-1.0,
+            )
+
+        def quantise(i):
+            nc.vector.quantize_mx(
+                out=q_w[:, i, :].bitcast(E5M2X4), scales=q_s[i][:], in_=woven[i][:].rearrange("p c t -> p (c t)")
+            )
+
+        g_w.append(sb.tile([P, J], U16, name="g_w1", tag="xt_w0", align_bytes=64))
+        nc.vector.tensor_copy(g_w[1][:], xt_w[1][:].indirect(idx[:]))
+        q_w = sb.tile([P, TILES, P], I32, name="q_w", tag="xt_w1", align_bytes=64)
+        quantise(0)
+        quantise(1)
 
         bi_ps = ps.tile([P, 2, P], F32, name="bi_ps")
         for c in range(2):
@@ -76,42 +121,11 @@ def tile_list_rows_othertable_gapoverpeak_kernel(
         bi_all = sb.tile([P, P, 2], F32, name="bi_all")
         nc.scalar.activation(bi_all[:], bi_ps[:].rearrange("q c p -> q p c"), COPY)
 
-        g_s = [sb.tile([P, J], U8, name="g_s%d" % z, align_bytes=64) for z in range(PASSES)]
-        g_x = sb.tile([P, PACK, J], F32, name="g_x", align_bytes=64)
-        woven = [sb.tile([P, P, PACK], BF16, name="woven%d" % i, align_bytes=64) for i in range(TILES)]
-        q_w = [sb.tile([P, P], I32, name="q_w%d" % i, align_bytes=64) for i in range(TILES)]
-        q_s = [sb.tile([P, P], U8, name="q_s%d" % i, align_bytes=64) for i in range(TILES)]
-
-        nc.vector.tensor_copy(g_x[:, 1, :], xs_sb[0][:, 1, :].indirect(idx2[:]))
-        for z in range(PASSES):
-            nc.vector.tensor_copy(g_s[z][:], xt_s[:, z, :].indirect(idx[:]))
-        for t in (0, 2, 3):
-            nc.scalar.activation(g_x[:, t, :], xs_sb[t // 2][:, t % 2, :].indirect(idx2[:]), COPY)
-        g_w = [
-            sb.tile([P, J], U16, name="g_w0", tag="reused", align_bytes=64),
-            sb.tile([P, J], U16, name="g_w1", align_bytes=64),
-        ]
-        nc.vector.tensor_copy(g_w[0][:], xt_w[0][:].indirect(idx[:]))
+        rs3 = sb.tile([P, TILES, N], F32, name="rs3", tag="g_x", align_bytes=64)
         for i in range(TILES):
-            nc.scalar.copy(
-                woven[i][:].rearrange("p (c u) t -> p c t u", u=4),
-                g_x[:, :, i * P : (i + 1) * P].rearrange("p t (c u) -> p c t u", u=4),
-            )
-
-        def quantise(i):
-            nc.vector.quantize_mx(
-                out=q_w[i][:].bitcast(E5M2X4), scales=q_s[i][:], in_=woven[i][:].rearrange("p c t -> p (c t)")
-            )
-
-        nc.vector.tensor_copy(g_w[1][:], xt_w[1][:].indirect(idx[:]))
-        quantise(0)
-        quantise(1)
-
-        rs3 = sb.tile([P, TILES, N], F32, name="rs3")
-        nc.scalar.activation(rs3[:], rs_sb[:], COPY, scale=0.3)
+            nc.scalar.activation(rs3[:, i, :], rs_sb[:, i, :], COPY, scale=0.3)
 
         a_ps = [ps.tile([P, N], F32, name="a_ps%d" % i) for i in range(TILES)]
-        b_ps = [ps.tile([P, N], F32, name="b_ps%d" % i) for i in range(TILES)]
 
         def pass_a(i, z):
             nc.tensor.matmul_mx(
@@ -119,29 +133,28 @@ def tile_list_rows_othertable_gapoverpeak_kernel(
                 lhsT=g_w[z][:, i * P : (i + 1) * P].bitcast(FP4X4),
                 lhsT_scale=g_s[z][:, i * P : (i + 1) * P],
                 rhs=wa_w[:, z, :].bitcast(FP4X4),
-                rhs_scale=w_s[:, z, :],
+                rhs_scale=wa_s[:, z, :],
                 start=(z == 0),
-                stop=(z == PASSES - 1),
+                stop=False,
             )
 
         def pass_b(i):
             nc.tensor.matmul_mx(
-                out=b_ps[i][:],
-                lhsT=q_w[i][:].bitcast(E5M2X4),
+                out=a_ps[i][:],
+                lhsT=q_w[:, i, :].bitcast(E5M2X4),
                 lhsT_scale=q_s[i][:],
                 rhs=wb_w[:].bitcast(E5M2X4),
-                rhs_scale=w_s[:, PASSES, :],
-                start=True,
+                rhs_scale=wb_s[:, 0, :],
+                start=False,
                 stop=True,
             )
 
-        for z in range(PASSES):
-            for i in range(TILES):
-                pass_a(i, z)
         for i in range(TILES):
+            pass_a(i, 0)
+        for i in range(TILES):
+            pass_a(i, 1)
             pass_b(i)
 
-        b2 = [sb.tile([P, N], F32, name="b2_%d" % i) for i in range(TILES)]
         d = [sb.tile([P, N], F32, name="d%d" % i) for i in range(TILES)]
         y = [sb.tile([P, N], F32, name="y%d" % i) for i in range(TILES)]
         peak = [sb.tile([P, 1], F32, name="peak%d" % i) for i in range(TILES)]
@@ -150,8 +163,7 @@ def tile_list_rows_othertable_gapoverpeak_kernel(
 
         def steps(i):
             return [
-                lambda: nc.vector.tensor_tensor(b2[i][:], a_ps[i][:], bi_all[:].rearrange("q p c -> q (p c)"), ALU.subtract),
-                lambda: nc.vector.tensor_tensor(d[i][:], b2[i][:], b_ps[i][:], ALU.subtract),
+                lambda: nc.vector.tensor_tensor(d[i][:], a_ps[i][:], bi_all[:].rearrange("q p c -> q (p c)"), ALU.subtract),
                 lambda: nc.vector.tensor_reduce(
                     peak[i][:], d[i][:], mybir.AxisListType.X, ALU.max, apply_absolute_value=True
                 ),

@@ -32,7 +32,7 @@ def tile_list_rows_othertable_gapoverpeak_kernel(
 
         idx = sb.tile([P, J // 16], U16, name="idx")
         idx2 = sb.tile([P, J // 16], U16, name="idx2")
-        xt_s = sb.tile([P, PASSES, T], U8, name="xt_s", align_bytes=64)
+        xt_s = sb.tile([P, PASSES, T], U8, name="xt_s", tag="xt_s", align_bytes=64)
         xt_w = [sb.tile([P, T], U16, name="xt_w%d" % z, tag="xt_w%d" % z, align_bytes=64) for z in range(PASSES)]
         xs_sb = [sb.tile([P, 2, S], F32, name="xs_sb%d" % h, tag="xs_sb%d" % h, align_bytes=64) for h in range(2)]
         wa_w = sb.tile([P, PASSES, 2 * N], U8, name="wa_w", align_bytes=64)
@@ -67,6 +67,7 @@ def tile_list_rows_othertable_gapoverpeak_kernel(
         nc.scalar.dma_start(out=xs_sb[0][:], in_=xs_rows[:, 0:2, :])
         nc.gpsimd.dma_start(out=xt_w[0][:].bitcast(I32), in_=xt_words[0].bitcast(I32))
         nc.gpsimd.dma_start(out=xt_w[1][:].bitcast(I32), in_=xt_words[1].bitcast(I32))
+        nc.gpsimd.dma_start(out=wb_w[:], in_=wb_words[0].rearrange("p n t -> p (n t)").bitcast(I32))
         nc.gpsimd.dma_start(out=rs_sb[:], in_=rs.rearrange("(i p) n -> p i n", p=P))
 
         nc.sync.dma_start(idx2[:], offs2)
@@ -80,7 +81,6 @@ def tile_list_rows_othertable_gapoverpeak_kernel(
         nc.sync.dma_start(out=wa_w[:].bitcast(I32), in_=wa_words.rearrange("z p c -> p z c").bitcast(I32))
         for r in range(2, 4):
             load_scale_row(wa_s, wa_scales, r)
-        nc.sync.dma_start(out=wb_w[:], in_=wb_words[0].rearrange("p n t -> p (n t)").bitcast(I32))
         for r in range(4):
             load_scale_row(wb_s, wb_scales, r)
 
@@ -89,20 +89,20 @@ def tile_list_rows_othertable_gapoverpeak_kernel(
         woven = [sb.tile([P, P, PACK], BF16, name="woven%d" % i, align_bytes=64) for i in range(TILES)]
         q_s = [sb.tile([P, P], U8, name="q_s%d" % i, align_bytes=64) for i in range(TILES)]
 
-        for t in range(3):
+        for t in range(PACK):
             nc.scalar.activation(g_x[:, t, :], xs_sb[t // 2][:, t % 2, :].indirect(idx2[:]), COPY)
         for z in range(PASSES):
             nc.vector.tensor_copy(g_s[z][:], xt_s[:, z, :].indirect(idx[:]))
-        nc.vector.tensor_copy(g_x[:, 3, :], xs_sb[1][:, 1, :].indirect(idx2[:]))
-        g_w = [sb.tile([P, J], U16, name="g_w0", tag="xs_sb1", align_bytes=64)]
+        g_w = [sb.tile([P, J], U16, name="g_w0", tag="xt_s", align_bytes=64)]
         nc.vector.tensor_copy(g_w[0][:], xt_w[0][:].indirect(idx[:]))
-        for i in range(TILES):
-            nc.scalar.activation(
+
+        def weave_views(i):
+            return (
                 woven[i][:].rearrange("p (c u) t -> p c t u", u=4),
                 g_x[:, :, i * P : (i + 1) * P].rearrange("p t (c u) -> p c t u", u=4),
-                COPY,
-                scale=-1.0,
             )
+
+        nc.scalar.activation(*weave_views(0), COPY, scale=-1.0)
 
         def quantise(i):
             nc.vector.quantize_mx(
@@ -111,6 +111,7 @@ def tile_list_rows_othertable_gapoverpeak_kernel(
 
         g_w.append(sb.tile([P, J], U16, name="g_w1", tag="xt_w0", align_bytes=64))
         nc.vector.tensor_copy(g_w[1][:], xt_w[1][:].indirect(idx[:]))
+        nc.vector.tensor_scalar(*weave_views(1), -1.0, None, ALU.mult)
         q_w = sb.tile([P, TILES, P], I32, name="q_w", tag="xt_w1", align_bytes=64)
         quantise(0)
         quantise(1)

from contextlib import ExitStack

import concourse.mybir as mybir

K, T, J, N, S, L = 1024, 1024, 256, 256, 512, 512
FLOPS = 2 * J * N * (K + L)

F32 = mybir.dt.float32
BF16 = mybir.dt.bfloat16
I32 = mybir.dt.int32
U16 = mybir.dt.uint16
U8 = mybir.dt.uint8
FP4X4 = mybir.dt.float4_e2m1fn_x4
E5M2X4 = mybir.dt.float8_e5m2_x4
ALU = mybir.AluOpType
ACT = mybir.ActivationFunctionType
COPY = ACT.Copy

P = 128
PACK = 4
PASSES = K // (P * PACK)
TILES = J // P


def tile_list_rows_othertable_gapoverpeak_kernel(
    tc, xt_words, xt_scales, wa_words, wa_scales, xs, wb_words, wb_scales, bi, rs, offs, offs2, out
):
    nc = tc.nc
    with ExitStack() as ctx:
        sb = ctx.enter_context(tc.tile_pool(name="sb", bufs=1))
        ps = ctx.enter_context(tc.psum_pool(name="ps", bufs=1))

        idx = sb.tile([P, J // 16], U16, name="idx")
        idx2 = sb.tile([P, J // 16], U16, name="idx2")
        xt_s = sb.tile([P, PASSES, T], U8, name="xt_s", tag="xt_s", align_bytes=64)
        xt_w = [sb.tile([P, T], U16, name="xt_w%d" % z, tag="xt_w%d" % z, align_bytes=64) for z in range(PASSES)]
        xs_sb = [sb.tile([P, 2, S], F32, name="xs_sb%d" % h, tag="xs_sb%d" % h, align_bytes=64) for h in range(2)]
        wa_w = sb.tile([P, PASSES, 2 * N], U8, name="wa_w", align_bytes=64)
        wa_s = sb.tile([P, PASSES, N], U8, name="wa_s", align_bytes=64)
        wb_s = sb.tile([P, 1, N], U8, name="wb_s", align_bytes=64)
        wb_w = sb.tile([P, N], I32, name="wb_w", align_bytes=64)
        bi_col = sb.tile([P, 2], F32, name="bi_col")
        rs_sb = sb.tile([P, TILES, N], F32, name="rs_sb")
        zero = sb.tile([P, 1], F32, name="zero")
        ident = sb.tile([P, P], F32, name="ident")

        nc.vector.memset(xt_s[:].bitcast(I32), 0)
        nc.gpsimd.memset(zero[:], 0.0)
        nc.gpsimd.memset(wa_s[:].bitcast(I32), 0)
        nc.gpsimd.memset(wb_s[:].bitcast(I32), 0)
        nc.scalar.activation(ident[:], zero[:].to_broadcast([P, P]), COPY)
        ones = sb.tile([P, 32], F32, name="ones")
        col = sb.tile([P, 32], F32, name="col", align_bytes=64)
        row = sb.tile([P, 32], F32, name="row", align_bytes=64)
        nc.vector.memset(ones[:], 1.0)
        nc.vector.tensor_tensor_scan(col[:], ones[:], ones[:], 0.0, ALU.mult, ALU.add)
        nc.vector.transpose(row[:], col[:])
        for q in range(4):
            part = slice(32 * q, 32 * q + 32)
            nc.vector.tensor_tensor(ident[part, part], col[part, :], row[part, :], ALU.is_equal)

        def load_scale_row(plane, scales, r):
            rows = scales.rearrange("z (q r) c -> r q z c", r=4)
            nc.sync.dma_start(out=plane[r:P:32].bitcast(I32), in_=rows[r].bitcast(I32))

        xs_rows = xs.rearrange("(p t) s -> p t s", t=PACK)
        nc.scalar.dma_start(out=xs_sb[0][:], in_=xs_rows[:, 0:2, :])
        nc.gpsimd.dma_start(out=xt_w[0][:].bitcast(I32), in_=xt_words[0].bitcast(I32))
        nc.gpsimd.dma_start(out=xt_w[1][:].bitcast(I32), in_=xt_words[1].bitcast(I32))
        nc.gpsimd.dma_start(out=wb_w[:], in_=wb_words[0].rearrange("p n t -> p (n t)").bitcast(I32))
        nc.gpsimd.dma_start(out=rs_sb[:], in_=rs.rearrange("(i p) n -> p i n", p=P))

        nc.sync.dma_start(idx2[:], offs2)
        nc.sync.dma_start(idx[:], offs)
        for r in range(4):
            load_scale_row(xt_s, xt_scales, r)
        nc.sync.dma_start(out=xs_sb[1][:], in_=xs_rows[:, 2:4, :])
        nc.sync.dma_start(out=bi_col[:], in_=bi[0].rearrange("(p c) -> p c", c=2))
        for r in range(2):
            load_scale_row(wa_s, wa_scales, r)
        nc.sync.dma_start(out=wa_w[:].bitcast(I32), in_=wa_words.rearrange("z p c -> p z c").bitcast(I32))
        for r in range(2, 4):
            load_scale_row(wa_s, wa_scales, r)
        for r in range(4):
            load_scale_row(wb_s, wb_scales, r)

        g_s = [sb.tile([P, J], U8, name="g_s%d" % z, align_bytes=64) for z in range(PASSES)]
        g_x = sb.tile([P, PACK, J], F32, name="g_x", tag="g_x", align_bytes=64)
        woven = [sb.tile([P, P, PACK], BF16, name="woven%d" % i, align_bytes=64) for i in range(TILES)]
        q_s = [sb.tile([P, P], U8, name="q_s%d" % i, align_bytes=64) for i in range(TILES)]

        for t in range(PACK):
            nc.scalar.activation(g_x[:, t, :], xs_sb[t // 2][:, t % 2, :].indirect(idx2[:]), COPY)
        for z in range(PASSES):
            nc.vector.tensor_copy(g_s[z][:], xt_s[:, z, :].indirect(idx[:]))
        g_w = [sb.tile([P, J], U16, name="g_w0", tag="xt_s", align_bytes=64)]
        nc.vector.tensor_copy(g_w[0][:], xt_w[0][:].indirect(idx[:]))

        def weave_views(i):
            return (
                woven[i][:].rearrange("p (c u) t -> p c t u", u=4),
                g_x[:, :, i * P : (i + 1) * P].rearrange("p t (c u) -> p c t u", u=4),
            )

        nc.scalar.activation(*weave_views(0), COPY, scale=-1.0)

        def quantise(i):
            nc.vector.quantize_mx(
                out=q_w[:, i, :].bitcast(E5M2X4), scales=q_s[i][:], in_=woven[i][:].rearrange("p c t -> p (c t)")
            )

        g_w.append(sb.tile([P, J], U16, name="g_w1", tag="xt_w0", align_bytes=64))
        nc.vector.tensor_copy(g_w[1][:], xt_w[1][:].indirect(idx[:]))
        nc.vector.tensor_scalar(*weave_views(1), -1.0, None, ALU.mult)
        q_w = sb.tile([P, TILES, P], I32, name="q_w", tag="xt_w1", align_bytes=64)
        quantise(0)
        quantise(1)

        bi_ps = ps.tile([P, 2, P], F32, name="bi_ps")
        for c in range(2):
            nc.tensor.transpose(bi_ps[:, c, :], bi_col[:, c : c + 1].to_broadcast([P, P]), ident[:])
        bi_all = sb.tile([P, P, 2], F32, name="bi_all")
        nc.scalar.activation(bi_all[:], bi_ps[:].rearrange("q c p -> q p c"), COPY)

        rs3 = sb.tile([P, TILES, N], F32, name="rs3", tag="g_x", align_bytes=64)
        for i in range(TILES):
            nc.scalar.activation(rs3[:, i, :], rs_sb[:, i, :], COPY, scale=0.3)

        a_ps = [ps.tile([P, N], F32, name="a_ps%d" % i) for i in range(TILES)]

        def pass_a(i, z):
            nc.tensor.matmul_mx(
                out=a_ps[i][:],
                lhsT=g_w[z][:, i * P : (i + 1) * P].bitcast(FP4X4),
                lhsT_scale=g_s[z][:, i * P : (i + 1) * P],
                rhs=wa_w[:, z, :].bitcast(FP4X4),
                rhs_scale=wa_s[:, z, :],
                start=(z == 0),
                stop=False,
            )

        def pass_b(i):
            nc.tensor.matmul_mx(
                out=a_ps[i][:],
                lhsT=q_w[:, i, :].bitcast(E5M2X4),
                lhsT_scale=q_s[i][:],
                rhs=wb_w[:].bitcast(E5M2X4),
                rhs_scale=wb_s[:, 0, :],
                start=False,
                stop=True,
            )

        for i in range(TILES):
            pass_a(i, 0)
        for i in range(TILES):
            pass_a(i, 1)
            pass_b(i)

        d = [sb.tile([P, N], F32, name="d%d" % i) for i in range(TILES)]
        y = [sb.tile([P, N], F32, name="y%d" % i) for i in range(TILES)]
        peak = [sb.tile([P, 1], F32, name="peak%d" % i) for i in range(TILES)]
        denom = [sb.tile([P, 1], F32, name="denom%d" % i) for i in range(TILES)]
        inv = [sb.tile([P, 1], F32, name="inv%d" % i) for i in range(TILES)]

        def steps(i):
            return [
                lambda: nc.vector.tensor_tensor(d[i][:], a_ps[i][:], bi_all[:].rearrange("q p c -> q (p c)"), ALU.subtract),
                lambda: nc.vector.tensor_reduce(
                    peak[i][:], d[i][:], mybir.AxisListType.X, ALU.max, apply_absolute_value=True
                ),
                lambda: nc.vector.tensor_scalar(denom[i][:], peak[i][:], 0.2, None, ALU.add),
                lambda: nc.vector.reciprocal(inv[i][:], denom[i][:]),
                lambda: nc.vector.scalar_tensor_tensor(
                    y[i][:], d[i][:], inv[i][:], rs3[:, i, :], ALU.mult, ALU.add
                ),
                lambda: nc.sync.dma_start(out=out[i * P : (i + 1) * P, :], in_=y[i][:]),
            ]

        for i in range(TILES):
            for step in steps(i):
                step()
